import numpy as np
import ml_dtypes


def mxq(x, axis, fmt="e4m3"):
    dtype, down = {"e4m3": (ml_dtypes.float8_e4m3fn, 7), "e5m2": (ml_dtypes.float8_e5m2, 14)}[fmt]
    v = np.moveaxis(np.asarray(x, np.float32).astype(ml_dtypes.bfloat16).astype(np.float64), axis, -1)
    blocks = v.reshape(v.shape[:-1] + (-1, 32))
    amax = np.abs(blocks).max(-1, keepdims=True)
    byte = np.maximum(np.where(amax > 0, np.frexp(amax)[1] - 1 + 127, 0) - down, 1)
    scale = np.exp2(byte - 127.0)
    codes = (blocks / scale).astype(np.float32).astype(dtype).astype(np.float64)
    return np.moveaxis((codes * scale).reshape(v.shape), -1, axis)


WIDE = False


def mx_kscale(k):
    if not WIDE:
        return np.ones(k)
    levels = np.array([10, -10, 5, -5, 0])
    if k % 512:
        return np.exp2(np.random.permutation(np.resize(levels, k // 32))).repeat(32)
    a = np.empty((k // 512, 16))
    for p in range(k // 512):
        a[p, :8] = np.random.permutation(np.resize(levels, 8))
        for g in range(8):
            far = levels[np.abs(levels - a[p, g]) >= 10]
            a[p, g + 8] = far[np.random.randint(len(far))]
    return np.exp2(a.ravel()).repeat(32)


def f64(x):
    return np.asarray(x).astype(np.float64)


def striped(idx):
    return np.tile(idx.reshape(-1, 16).T, (8, 1)).astype(np.uint16)


def unstriped(offs):
    return offs[:16].T.reshape(-1).astype(np.int64)


def pack_weight(w):
    k, n = w.shape
    w = f64(np.asarray(w, np.float32).astype(ml_dtypes.bfloat16)).reshape(k // 32, 32, n)
    amax = np.abs(w).max(1)
    byte = np.clip(np.where(amax > 0, np.frexp(amax)[1] - 1 + 127 - 7, 1), 1, 254)
    scaled = (w * np.exp2(127.0 - byte)[:, None, :]).reshape(k, n).astype(np.float32)
    words = np.ascontiguousarray(scaled.reshape(k // 512, 128, 4, n).transpose(0, 1, 3, 2)).astype(ml_dtypes.float8_e4m3fn).view(np.uint8)
    return words, np.ascontiguousarray(byte.astype(np.uint8).reshape(k // 512, 16, n))


def unpack_weight(words, scales):
    g, p, n, _ = words.shape
    vals = np.ascontiguousarray(words).view(ml_dtypes.float8_e4m3fn).astype(np.float64) * np.repeat(np.exp2(scales.astype(np.float64) - 127.0), 8, axis=1)[..., None]
    return vals.transpose(0, 1, 3, 2).reshape(g * 512, n)


def relu(v):
    return np.maximum(v, 0.0)


K, T, S, D, N = 512, 1024, 512, 4, 256
P = 2 ** 7


def setup_inputs():
    n = np.random.standard_normal
    s = mx_kscale(K)[:, None]
    packed_xT = pack_weight(n((K, T)) * s)
    packed_eT = pack_weight(n((K, T)) * s)
    packed_dT = pack_weight(n((K, T)) * s)
    return {
        "x_words": packed_xT[0],
        "x_scales": packed_xT[1],
        "e_words": packed_eT[0],
        "e_scales": packed_eT[1],
        "d_words": packed_dT[0],
        "d_scales": packed_dT[1],
        "w1": (n((K, N)) / np.sqrt(K) / s).astype(np.float32),
        "w2": (n((K, N)) / np.sqrt(K) / s).astype(np.float32),
        "dist": (np.tile(np.random.uniform(0.5, 2.0, S), (P, 1))).astype(np.float32),
        "use": (np.tile(np.random.uniform(0.5, 1.0, S), (P, 1))).astype(np.float32),
        "offs": striped(np.random.permutation(T)[:S]),
    }


def reference(x_words, x_scales, e_words, e_scales, d_words, d_scales, w1, w2, dist, use, offs):
    xq = unpack_weight(x_words, x_scales)[:, unstriped(offs)]
    f0 = mxq(f64(w1), 0, "e4m3").T @ xq
    e_offs = unpack_weight(e_words, e_scales)[:, unstriped(offs)]
    w2q = mxq(f64(w2), 0, "e4m3")
    c0 = w2q.T @ e_offs
    d_offs = unpack_weight(d_words, d_scales)[:, unstriped(offs)]
    c1 = w2q.T @ d_offs
    cost = ((np.abs(f0 - c0) + 0.3) * (np.abs(c1 - c0) + 0.3)) * f64(dist)[:1]
    iw = f64(use)[:1] / cost
    wf = iw * (f0 + c1 - c0)
    sw = iw.reshape(len(iw), -1, D).sum(axis=2)
    return relu((wf.reshape(len(wf), -1, D).sum(axis=2)) / sw)

@@ -1,0 +1,227 @@
+from contextlib import ExitStack
+
+import concourse.mybir as mybir
+from concourse.masks import make_identity
+
+K, T, S, D, N = 512, 1024, 512, 4, 256
+P = 128
+PACK = 4
+V = S // D
+HALVES = 2
+SH = S // HALVES
+VH = V // HALVES
+FLOOR = 0.3
+
+FLOPS = 3 * 2 * K * N * S
+BYTES = 3 * (P * T * PACK + 16 * T) + 2 * K * N * 4 + 2 * S * 4 + P * (S // 16) * 2 + N * V * 4
+
+F32 = mybir.dt.float32
+BF16 = mybir.dt.bfloat16
+I32 = mybir.dt.int32
+U32 = mybir.dt.uint32
+U16 = mybir.dt.uint16
+U8 = mybir.dt.uint8
+FP8X4 = mybir.dt.float8_e4m3fn_x4
+ACT = mybir.ActivationFunctionType
+ALU = mybir.AluOpType
+
+
+def tile_picked_ystarfm_relu_p_kernel(
+    tc, x_words, x_scales, e_words, e_scales, d_words, d_scales, w1, w2, dist, use, offs, out
+):
+    nc = tc.nc
+    with ExitStack() as ctx:
+        sb = ctx.enter_context(tc.tile_pool(name="sb", bufs=1))
+        ps = ctx.enter_context(tc.psum_pool(name="ps", bufs=1))
+
+        def bank(name, tag, width=512):
+            return ps.tile([P, width], F32, name=name, tag=tag)
+
+        def load_scales(name, scales):
+            t = sb.tile([P, T], U8, name=name, align_bytes=64)
+            nc.vector.memset(t[:].bitcast(I32), 0)
+            for q in range(4):
+                nc.sync.dma_start(out=t[32 * q : 32 * q + 4, :].bitcast(I32), in_=scales[0, 4 * q : 4 * q + 4, :].bitcast(I32))
+            return t
+
+        def load_words(name, words):
+            t = sb.tile([P, T], U32, name=name)
+            nc.sync.dma_start(out=t[:].bitcast(I32), in_=words[0].rearrange("p n t -> p (n t)").bitcast(I32))
+            return t
+
+        def load_weight(name, w):
+            t = sb.tile([P, PACK, N], F32, name=name)
+            nc.sync.dma_start(out=t[:], in_=w.rearrange("(p j) n -> p j n", j=PACK))
+            return t
+
+        def load_row(name, rows):
+            t = sb.tile([P, HALVES, D], F32, name=name)
+            for h in range(2):
+                nc.gpsimd.dma_start(out=t[h * VH : (h + 1) * VH], in_=rows[h].rearrange("(l v d) -> v l d", l=HALVES, d=D))
+            return t
+
+        def gather(name, table, dtype, first, count, after=None):
+            t = sb.tile([P, count], dtype, name=name, tag=after or name, align_bytes=64)
+            nc.vector.tensor_copy(t[:], table[:].indirect(offsets[:, first // 16 : (first + count) // 16]))
+            return t
+
+        def round_weight(name, raw):
+            t = sb.tile([P, N * PACK], BF16, name=name, align_bytes=64)
+            nc.scalar.copy(
+                out=t[:].rearrange("p (c i j) -> p c j i", i=4, j=PACK),
+                in_=raw[:].rearrange("p j (c i) -> p c j i", i=4),
+            )
+            return t
+
+        def round_weight_pool(name, raw):
+            t = sb.tile([P, N * PACK], BF16, name=name, align_bytes=64)
+            nc.gpsimd.tensor_scalar(
+                t[:].rearrange("p (n j) -> p n j", j=PACK), raw[:].rearrange("p j n -> p n j"), 1.0, 0.0, ALU.mult, ALU.add
+            )
+            return t
+
+        def quantise(name, rounded, after=None):
+            codes = sb.tile([P, N], U32, name=name + "_codes", tag=after or name + "_codes", align_bytes=64)
+            scales = sb.tile([P, N], U8, name=name + "_scales", align_bytes=64)
+            nc.vector.quantize_mx(out=codes[:].bitcast(FP8X4), scales=scales[:], in_=rounded[:])
+            return codes, scales
+
+        def product(name, tag, weight, words, scales):
+            b = bank(name, tag)
+            for h in range(2):
+                cols = slice(h * P, (h + 1) * P)
+                nc.tensor.matmul_mx(
+                    out=b[:, h * SH : (h + 1) * SH], lhsT=weight[0][:, cols].bitcast(FP8X4), lhsT_scale=weight[1][:, cols],
+                    rhs=words.bitcast(FP8X4), rhs_scale=scales, start=True, stop=True,
+                )
+            return b
+
+        def dealt(b):
+            return b[:].rearrange("p (u d) -> p d u", d=D)
+
+        def turn(dst, src, first, last, ds=range(D), at=0):
+            for d in ds:
+                nc.tensor.matmul(
+                    out=dst[:, (d - at) * P : (d - at + 1) * P], lhsT=src[:, d, :], rhs=ident[:], is_transpose=True,
+                    start=first and d == ds[0], stop=last and d == ds[-1],
+                )
+
+        def half(t, l):
+            return t[:, l * SH : (l + 1) * SH]
+
+        one = sb.tile([P, 1], F32, name="one")
+        warm = sb.tile([P, 1], F32, name="warm")
+        nc.gpsimd.memset(one[:], 1.0)
+        nc.scalar.activation(warm[:], one[:], ACT.Abs_reciprocal_sqrt)
+        dist_v = load_row("dist_v", dist)
+        use_v = load_row("use_v", use)
+        ew = load_words("ew", e_words)
+        offsets = sb.tile([P, S // 16], U16, name="offsets")
+        nc.sync.dma_start(offsets[:], offs)
+        es = load_scales("es", e_scales)
+        w2raw = load_weight("w2raw", w2)
+        dw = load_words("dw", d_words)
+        ds = load_scales("ds", d_scales)
+        w1raw = load_weight("w1raw", w1)
+        xw = load_words("xw", x_words)
+        xs = load_scales("xs", x_scales)
+        ident = sb.tile([P, P], F32, name="ident")
+        make_identity(nc, ident[:])
+
+        ewg = gather("ewg", ew, U32, 0, S)
+        esg = gather("esg", es, U8, 0, S)
+        w2q = quantise("w2", round_weight("w2r", w2raw))
+        droot = sb.tile([P, HALVES, D], F32, name="droot", tag="w2raw")
+        dinv = sb.tile([P, HALVES, D], F32, name="dinv")
+        usign = sb.tile([P, HALVES, D], F32, name="usign")
+        r = sb.tile([P, HALVES, D], F32, name="r")
+        nc.scalar.activation(droot[:], dist_v[:], ACT.Abs_reciprocal_sqrt)
+        nc.scalar.activation(dinv[:], droot[:], ACT.Square)
+        nc.scalar.activation(droot[:], dist_v[:], ACT.Sign)
+        nc.gpsimd.tensor_tensor(usign[:], use_v[:], droot[:], ALU.mult)
+        nc.gpsimd.tensor_tensor(r[:], usign[:], dinv[:], ALU.mult)
+
+        c0 = [product(f"c0_{l}", f"A{l}", w2q, half(ewg, l), half(esg, l)) for l in range(HALVES)]
+        dwg0 = gather("dwg0", dw, U32, 0, SH, "w2r")
+        dsg = gather("dsg", ds, U8, 0, S)
+        dwg1 = gather("dwg1", dw, U32, SH, SH, "ds")
+        c1 = [product(f"c1_{l}", f"B{l}", w2q, g[:], half(dsg, l)) for l, g in enumerate((dwg0, dwg1))]
+        w1r = round_weight("w1r", w1raw)
+        w1q = quantise("w1", w1r)
+        xwg0 = gather("xwg0", xw, U32, 0, SH)
+        xsg0 = gather("xsg0", xs, U8, 0, SH)
+        xsg1 = gather("xsg1", xs, U8, SH, SH)
+        xwg1 = gather("xwg1", xw, U32, SH, SH, "xs")
+        bT = [bank(f"bT{l}", f"C{l}") for l in range(HALVES)]
+        sT = [bank(f"sT{l}", f"D{l}") for l in range(HALVES)]
+        n0, c1s = [], []
+        for l in range(HALVES):
+            t = sb.tile([P, D, P], F32, name=f"n0_{l}")
+            nc.scalar.activation(t[:], dealt(c0[l]), ACT.Copy, scale=-1.0)
+            n0.append(t)
+            turn(bT[l], t, True, False)
+            t = sb.tile([P, D, P], F32, name=f"c1s_{l}")
+            nc.scalar.copy(t[:], dealt(c1[l]))
+            c1s.append(t)
+            turn(bT[l], t, False, True)
+        f0 = [product(f"f0_{l}", f"A{l}", w1q, g[:], s[:]) for l, (g, s) in enumerate(((xwg0, xsg0), (xwg1, xsg1)))]
+        for l in range(HALVES):
+            turn(sT[l], c1s[l], True, False)
+        yb = []
+        for l in range(HALVES):
+            ab = sb.tile([P, S], F32, name=f"ab_{l}")
+            nc.scalar.activation(ab[:], bT[l][:], ACT.Abs)
+            t = sb.tile([P, S], F32, name=f"yb_{l}")
+            nc.scalar.activation(t[:], ab[:], ACT.Abs_reciprocal_sqrt, bias=FLOOR)
+            yb.append(t)
+        a, aT = [], []
+        PAIRS = 2
+        W = D // PAIRS
+        for l in range(HALVES):
+            t = sb.tile([P, D, P], F32, name=f"a_{l}")
+            for g in range(PAIRS):
+                ds_ = range(g * W, (g + 1) * W)
+                nc.vector.tensor_tensor(t[:, g * W : (g + 1) * W], dealt(f0[l])[:, g * W : (g + 1) * W], n0[l][:, g * W : (g + 1) * W], ALU.add)
+                b = bank(f"aT{l}_{g}", f"{'BC'[l]}{g}", W * P)
+                turn(b, t, True, True, ds_, g * W)
+                aT.append(b)
+            a.append(t)
+            turn(sT[l], t, False, True)
+        sums = []
+        for l in range(HALVES):
+            iw = sb.tile([P, S], F32, name=f"iw_{l}")
+            wf = sb.tile([P, S], F32, name=f"wf_{l}")
+            for g in range(PAIRS):
+                gc = slice(g * W * P, (g + 1) * W * P)
+                aa = sb.tile([P, W * P], F32, name=f"aa_{l}_{g}")
+                nc.scalar.activation(aa[:], aT[l * PAIRS + g][:], ACT.Abs)
+                ya = sb.tile([P, W * P], F32, name=f"ya_{l}_{g}")
+                nc.scalar.activation(ya[:], aa[:], ACT.Abs_reciprocal_sqrt, bias=FLOOR)
+                z = sb.tile([P, W * P], F32, name=f"z_{l}_{g}")
+                nc.vector.tensor_tensor(z[:], ya[:], yb[l][:, gc], ALU.mult)
+                for e in range(W):
+                    d = g * W + e
+                    zc = z[:, e * P : (e + 1) * P]
+                    nc.vector.scalar_tensor_tensor(iw[:, d * P : (d + 1) * P], zc, r[:, l, d : d + 1], zc, ALU.mult, ALU.mult)
+                nc.vector.tensor_tensor(wf[:, gc], sT[l][:, gc], iw[:, gc], ALU.mult)
+            den = bank(f"den{l}", f"A{l}", P)
+            num = bank(f"num{l}", f"B{l}", P)
+            for dst, src in ((den, iw), (num, wf)):
+                for d in range(D):
+                    nc.tensor.matmul(out=dst[:], lhsT=src[:, d * P : (d + 1) * P], rhs=ident[:], is_transpose=True,
+                                     start=d == 0, stop=d == D - 1)
+            sums.append((den, num))
+        out_v = out.rearrange("(h m) v -> m h v", h=2)
+        for l in range(HALVES):
+            den, num = sums[l]
+            sg = sb.tile([P, P], F32, name=f"sg_{l}")
+            y = sb.tile([P, P], F32, name=f"y_{l}")
+            y2 = sb.tile([P, P], F32, name=f"y2_{l}")
+            nc.scalar.activation(sg[:], den[:], ACT.Sign)
+            nc.scalar.activation(y[:], den[:], ACT.Abs_reciprocal_sqrt)
+            nc.scalar.activation(y2[:], y[:], ACT.Square)
+            t = sb.tile([P, P], F32, name=f"t_{l}")
+            nc.vector.tensor_tensor(t[:], num[:], sg[:], ALU.mult)
+            o = sb.tile([P, P], F32, name=f"o_{l}")
+            nc.vector.scalar_tensor_tensor(o[:], t[:], 0.0, y2[:], ALU.max, ALU.mult)
+            nc.sync.dma_start(out=out_v[:, :, l * VH : (l + 1) * VH], in_=o[:].rearrange("p (h v) -> p h v", h=2))

@@ -45,7 +45,7 @@ def tile_picked_ystarfm_relu_p_kernel(
             return t
 
         def load_words(name, words):
-            t = sb.tile([P, T], U32, name=name)
+            t = sb.tile([P, T], U32, name=name, align_bytes=64)
             nc.sync.dma_start(out=t[:].bitcast(I32), in_=words[0].rearrange("p n t -> p (n t)").bitcast(I32))
             return t
 
@@ -120,9 +120,9 @@ def tile_picked_ystarfm_relu_p_kernel(
         nc.sync.dma_start(offsets[:], offs)
         es = load_scales("es", e_scales)
         w2raw = load_weight("w2raw", w2)
-        dw = load_words("dw", d_words)
-        ds = load_scales("ds", d_scales)
         w1raw = load_weight("w1raw", w1)
+        ds = load_scales("ds", d_scales)
+        dw = load_words("dw", d_words)
         xw = load_words("xw", x_words)
         xs = load_scales("xs", x_scales)
         ident = sb.tile([P, P], F32, name="ident")
@@ -131,26 +131,15 @@ def tile_picked_ystarfm_relu_p_kernel(
         ewg = gather("ewg", ew, U32, 0, S)
         esg = gather("esg", es, U8, 0, S)
         w2q = quantise("w2", round_weight("w2r", w2raw))
-        droot = sb.tile([P, HALVES, D], F32, name="droot", tag="w2raw")
-        dinv = sb.tile([P, HALVES, D], F32, name="dinv")
-        usign = sb.tile([P, HALVES, D], F32, name="usign")
-        r = sb.tile([P, HALVES, D], F32, name="r")
-        nc.scalar.activation(droot[:], dist_v[:], ACT.Abs_reciprocal_sqrt)
-        nc.scalar.activation(dinv[:], droot[:], ACT.Square)
-        nc.scalar.activation(droot[:], dist_v[:], ACT.Sign)
-        nc.gpsimd.tensor_tensor(usign[:], use_v[:], droot[:], ALU.mult)
-        nc.gpsimd.tensor_tensor(r[:], usign[:], dinv[:], ALU.mult)
-
         c0 = [product(f"c0_{l}", f"A{l}", w2q, half(ewg, l), half(esg, l)) for l in range(HALVES)]
-        dwg0 = gather("dwg0", dw, U32, 0, SH, "w2r")
-        dsg = gather("dsg", ds, U8, 0, S)
-        dwg1 = gather("dwg1", dw, U32, SH, SH, "ds")
-        c1 = [product(f"c1_{l}", f"B{l}", w2q, g[:], half(dsg, l)) for l, g in enumerate((dwg0, dwg1))]
         w1r = round_weight("w1r", w1raw)
-        w1q = quantise("w1", w1r)
+        dsg = gather("dsg", ds, U8, 0, S)
+        dwg0 = gather("dwg0", dw, U32, 0, SH)
+        dwg1 = gather("dwg1", dw, U32, SH, SH)
+        c1 = [product(f"c1_{l}", f"B{l}", w2q, g[:], half(dsg, l)) for l, g in enumerate((dwg0, dwg1))]
+        w1q = quantise("w1", w1r, "dw")
         xwg0 = gather("xwg0", xw, U32, 0, SH)
-        xsg0 = gather("xsg0", xs, U8, 0, SH)
-        xsg1 = gather("xsg1", xs, U8, SH, SH)
+        xsg = gather("xsg", xs, U8, 0, S)
         xwg1 = gather("xwg1", xw, U32, SH, SH, "xs")
         bT = [bank(f"bT{l}", f"C{l}") for l in range(HALVES)]
         sT = [bank(f"sT{l}", f"D{l}") for l in range(HALVES)]
@@ -159,21 +148,31 @@ def tile_picked_ystarfm_relu_p_kernel(
             t = sb.tile([P, D, P], F32, name=f"n0_{l}")
             nc.scalar.activation(t[:], dealt(c0[l]), ACT.Copy, scale=-1.0)
             n0.append(t)
-            turn(bT[l], t, True, False)
+        for l in range(HALVES):
             t = sb.tile([P, D, P], F32, name=f"c1s_{l}")
             nc.scalar.copy(t[:], dealt(c1[l]))
             c1s.append(t)
-            turn(bT[l], t, False, True)
-        f0 = [product(f"f0_{l}", f"A{l}", w1q, g[:], s[:]) for l, (g, s) in enumerate(((xwg0, xsg0), (xwg1, xsg1)))]
-        for l in range(HALVES):
-            turn(sT[l], c1s[l], True, False)
-        yb = []
+        turn(bT[0], n0[0], True, False)
+        turn(bT[0], c1s[0], False, True)
+        turn(bT[1], c1s[1], True, False)
+        turn(bT[1], n0[1], False, True)
+        f0 = [product(f"f0_{l}", f"A{l}", w1q, g[:], half(xsg, l)) for l, g in enumerate((xwg0, xwg1))]
+        ub = []
         for l in range(HALVES):
             ab = sb.tile([P, S], F32, name=f"ab_{l}")
             nc.scalar.activation(ab[:], bT[l][:], ACT.Abs)
-            t = sb.tile([P, S], F32, name=f"yb_{l}")
-            nc.scalar.activation(t[:], ab[:], ACT.Abs_reciprocal_sqrt, bias=FLOOR)
-            yb.append(t)
+            t = sb.tile([P, S], F32, name=f"ub_{l}")
+            nc.gpsimd.tensor_scalar(t[:], ab[:], 1.0, FLOOR, ALU.mult, ALU.add)
+            ub.append(t)
+        parts = sb.tile([P, 2, HALVES, D], F32, name="parts", tag="ab_0")
+        dinv = sb.tile([P, HALVES, D], F32, name="dinv")
+        usign = sb.tile([P, HALVES, D], F32, name="usign")
+        r = sb.tile([P, HALVES, D], F32, name="r")
+        nc.scalar.activation(parts[:, 0], dist_v[:], ACT.Abs_reciprocal_sqrt)
+        nc.scalar.activation(parts[:, 1], dist_v[:], ACT.Sign)
+        nc.scalar.activation(dinv[:], parts[:, 0], ACT.Square)
+        nc.gpsimd.tensor_tensor(usign[:], use_v[:], parts[:, 1], ALU.mult)
+        nc.gpsimd.tensor_tensor(r[:], usign[:], dinv[:], ALU.mult)
         a, aT = [], []
         PAIRS = 2
         W = D // PAIRS
@@ -186,39 +185,51 @@ def tile_picked_ystarfm_relu_p_kernel(
                 turn(b, t, True, True, ds_, g * W)
                 aT.append(b)
             a.append(t)
-            turn(sT[l], t, False, True)
-        sums = []
         for l in range(HALVES):
-            iw = sb.tile([P, S], F32, name=f"iw_{l}")
-            wf = sb.tile([P, S], F32, name=f"wf_{l}")
+            turn(sT[l], a[l], True, False)
+            turn(sT[l], c1s[l], False, True)
+        roots = []
+        for l in range(HALVES):
             for g in range(PAIRS):
                 gc = slice(g * W * P, (g + 1) * W * P)
                 aa = sb.tile([P, W * P], F32, name=f"aa_{l}_{g}")
                 nc.scalar.activation(aa[:], aT[l * PAIRS + g][:], ACT.Abs)
-                ya = sb.tile([P, W * P], F32, name=f"ya_{l}_{g}")
-                nc.scalar.activation(ya[:], aa[:], ACT.Abs_reciprocal_sqrt, bias=FLOOR)
+                cost = sb.tile([P, W * P], F32, name=f"cost_{l}_{g}")
+                nc.vector.scalar_tensor_tensor(cost[:], aa[:], FLOOR, ub[l][:, gc], ALU.add, ALU.mult)
                 z = sb.tile([P, W * P], F32, name=f"z_{l}_{g}")
-                nc.vector.tensor_tensor(z[:], ya[:], yb[l][:, gc], ALU.mult)
-                for e in range(W):
-                    d = g * W + e
-                    zc = z[:, e * P : (e + 1) * P]
-                    nc.vector.scalar_tensor_tensor(iw[:, d * P : (d + 1) * P], zc, r[:, l, d : d + 1], zc, ALU.mult, ALU.mult)
-                nc.vector.tensor_tensor(wf[:, gc], sT[l][:, gc], iw[:, gc], ALU.mult)
-            den = bank(f"den{l}", f"A{l}", P)
-            num = bank(f"num{l}", f"B{l}", P)
-            for dst, src in ((den, iw), (num, wf)):
-                for d in range(D):
-                    nc.tensor.matmul(out=dst[:], lhsT=src[:, d * P : (d + 1) * P], rhs=ident[:], is_transpose=True,
-                                     start=d == 0, stop=d == D - 1)
-            sums.append((den, num))
+                nc.scalar.activation(z[:], cost[:], ACT.Abs_reciprocal_sqrt)
+                roots.append(z)
+
+        def add_up(name, tag, src):
+            dst = bank(name, tag, P)
+            for d in range(D):
+                nc.tensor.matmul(out=dst[:], lhsT=src[:, d * P : (d + 1) * P], rhs=ident[:], is_transpose=True,
+                                 start=d == 0, stop=d == D - 1)
+            return dst
+
+        iws, dens, nums = [], [], []
+        for l in range(HALVES):
+            iw = sb.tile([P, S], F32, name=f"iw_{l}")
+            for d in range(D):
+                zc = roots[l * PAIRS + d // W][:, (d % W) * P : (d % W + 1) * P]
+                nc.vector.scalar_tensor_tensor(iw[:, d * P : (d + 1) * P], zc, r[:, l, d : d + 1], zc, ALU.mult, ALU.mult)
+            iws.append(iw)
+            dens.append(add_up(f"den{l}", f"A{l}", iw))
+        for l in range(HALVES):
+            wf = sb.tile([P, S], F32, name=f"wf_{l}")
+            for g in range(l + 1):
+                gc = slice(g * S // (l + 1), (g + 1) * S // (l + 1))
+                nc.vector.tensor_tensor(wf[:, gc], sT[l][:, gc], iws[l][:, gc], ALU.mult)
+            nums.append(add_up(f"num{l}", f"B{l}", wf))
+        sums = list(zip(dens, nums))
         out_v = out.rearrange("(h m) v -> m h v", h=2)
         for l in range(HALVES):
             den, num = sums[l]
             sg = sb.tile([P, P], F32, name=f"sg_{l}")
             y = sb.tile([P, P], F32, name=f"y_{l}")
             y2 = sb.tile([P, P], F32, name=f"y2_{l}")
-            nc.scalar.activation(sg[:], den[:], ACT.Sign)
             nc.scalar.activation(y[:], den[:], ACT.Abs_reciprocal_sqrt)
+            nc.scalar.activation(sg[:], den[:], ACT.Sign)
             nc.scalar.activation(y2[:], y[:], ACT.Square)
             t = sb.tile([P, P], F32, name=f"t_{l}")
             nc.vector.tensor_tensor(t[:], num[:], sg[:], ALU.mult)

from contextlib import ExitStack

import concourse.mybir as mybir
from concourse.masks import make_identity

K, T, S, D, N = 512, 1024, 512, 4, 256
P = 128
PACK = 4
V = S // D
HALVES = 2
SH = S // HALVES
VH = V // HALVES
FLOOR = 0.3

FLOPS = 3 * 2 * K * N * S
BYTES = 3 * (P * T * PACK + 16 * T) + 2 * K * N * 4 + 2 * S * 4 + P * (S // 16) * 2 + N * V * 4

F32 = mybir.dt.float32
BF16 = mybir.dt.bfloat16
I32 = mybir.dt.int32
U32 = mybir.dt.uint32
U16 = mybir.dt.uint16
U8 = mybir.dt.uint8
FP8X4 = mybir.dt.float8_e4m3fn_x4
ACT = mybir.ActivationFunctionType
ALU = mybir.AluOpType


def tile_picked_ystarfm_relu_p_kernel(
    tc, x_words, x_scales, e_words, e_scales, d_words, d_scales, w1, w2, dist, use, offs, out
):
    nc = tc.nc
    with ExitStack() as ctx:
        sb = ctx.enter_context(tc.tile_pool(name="sb", bufs=1))
        ps = ctx.enter_context(tc.psum_pool(name="ps", bufs=1))

        def bank(name, tag, width=512):
            return ps.tile([P, width], F32, name=name, tag=tag)

        def load_scales(name, scales):
            t = sb.tile([P, T], U8, name=name, align_bytes=64)
            nc.vector.memset(t[:].bitcast(I32), 0)
            for q in range(4):
                nc.sync.dma_start(out=t[32 * q : 32 * q + 4, :].bitcast(I32), in_=scales[0, 4 * q : 4 * q + 4, :].bitcast(I32))
            return t

        def load_words(name, words):
            t = sb.tile([P, T], U32, name=name, align_bytes=64)
            nc.sync.dma_start(out=t[:].bitcast(I32), in_=words[0].rearrange("p n t -> p (n t)").bitcast(I32))
            return t

        def load_weight(name, w):
            t = sb.tile([P, PACK, N], F32, name=name)
            nc.sync.dma_start(out=t[:], in_=w.rearrange("(p j) n -> p j n", j=PACK))
            return t

        def load_row(name, rows):
            t = sb.tile([P, HALVES, D], F32, name=name)
            for h in range(2):
                nc.gpsimd.dma_start(out=t[h * VH : (h + 1) * VH], in_=rows[h].rearrange("(l v d) -> v l d", l=HALVES, d=D))
            return t

        def gather(name, table, dtype, first, count, after=None):
            t = sb.tile([P, count], dtype, name=name, tag=after or name, align_bytes=64)
            nc.vector.tensor_copy(t[:], table[:].indirect(offsets[:, first // 16 : (first + count) // 16]))
            return t

        def round_weight(name, raw):
            t = sb.tile([P, N * PACK], BF16, name=name, align_bytes=64)
            nc.scalar.copy(
                out=t[:].rearrange("p (c i j) -> p c j i", i=4, j=PACK),
                in_=raw[:].rearrange("p j (c i) -> p c j i", i=4),
            )
            return t

        def round_weight_pool(name, raw):
            t = sb.tile([P, N * PACK], BF16, name=name, align_bytes=64)
            nc.gpsimd.tensor_scalar(
                t[:].rearrange("p (n j) -> p n j", j=PACK), raw[:].rearrange("p j n -> p n j"), 1.0, 0.0, ALU.mult, ALU.add
            )
            return t

        def quantise(name, rounded, after=None):
            codes = sb.tile([P, N], U32, name=name + "_codes", tag=after or name + "_codes", align_bytes=64)
            scales = sb.tile([P, N], U8, name=name + "_scales", align_bytes=64)
            nc.vector.quantize_mx(out=codes[:].bitcast(FP8X4), scales=scales[:], in_=rounded[:])
            return codes, scales

        def product(name, tag, weight, words, scales):
            b = bank(name, tag)
            for h in range(2):
                cols = slice(h * P, (h + 1) * P)
                nc.tensor.matmul_mx(
                    out=b[:, h * SH : (h + 1) * SH], lhsT=weight[0][:, cols].bitcast(FP8X4), lhsT_scale=weight[1][:, cols],
                    rhs=words.bitcast(FP8X4), rhs_scale=scales, start=True, stop=True,
                )
            return b

        def dealt(b):
            return b[:].rearrange("p (u d) -> p d u", d=D)

        def turn(dst, src, first, last, ds=range(D), at=0):
            for d in ds:
                nc.tensor.matmul(
                    out=dst[:, (d - at) * P : (d - at + 1) * P], lhsT=src[:, d, :], rhs=ident[:], is_transpose=True,
                    start=first and d == ds[0], stop=last and d == ds[-1],
                )

        def half(t, l):
            return t[:, l * SH : (l + 1) * SH]

        one = sb.tile([P, 1], F32, name="one")
        warm = sb.tile([P, 1], F32, name="warm")
        nc.gpsimd.memset(one[:], 1.0)
        nc.scalar.activation(warm[:], one[:], ACT.Abs_reciprocal_sqrt)
        dist_v = load_row("dist_v", dist)
        use_v = load_row("use_v", use)
        ew = load_words("ew", e_words)
        offsets = sb.tile([P, S // 16], U16, name="offsets")
        nc.sync.dma_start(offsets[:], offs)
        es = load_scales("es", e_scales)
        w2raw = load_weight("w2raw", w2)
        w1raw = load_weight("w1raw", w1)
        ds = load_scales("ds", d_scales)
        dw = load_words("dw", d_words)
        xw = load_words("xw", x_words)
        xs = load_scales("xs", x_scales)
        ident = sb.tile([P, P], F32, name="ident")
        make_identity(nc, ident[:])

        ewg = gather("ewg", ew, U32, 0, S)
        esg = gather("esg", es, U8, 0, S)
        w2q = quantise("w2", round_weight("w2r", w2raw))
        c0 = [product(f"c0_{l}", f"A{l}", w2q, half(ewg, l), half(esg, l)) for l in range(HALVES)]
        w1r = round_weight("w1r", w1raw)
        dsg = gather("dsg", ds, U8, 0, S)
        dwg0 = gather("dwg0", dw, U32, 0, SH)
        dwg1 = gather("dwg1", dw, U32, SH, SH)
        c1 = [product(f"c1_{l}", f"B{l}", w2q, g[:], half(dsg, l)) for l, g in enumerate((dwg0, dwg1))]
        w1q = quantise("w1", w1r, "dw")
        xwg0 = gather("xwg0", xw, U32, 0, SH)
        xsg = gather("xsg", xs, U8, 0, S)
        xwg1 = gather("xwg1", xw, U32, SH, SH, "xs")
        bT = [bank(f"bT{l}", f"C{l}") for l in range(HALVES)]
        sT = [bank(f"sT{l}", f"D{l}") for l in range(HALVES)]
        n0, c1s = [], []
        for l in range(HALVES):
            t = sb.tile([P, D, P], F32, name=f"n0_{l}")
            nc.scalar.activation(t[:], dealt(c0[l]), ACT.Copy, scale=-1.0)
            n0.append(t)
        for l in range(HALVES):
            t = sb.tile([P, D, P], F32, name=f"c1s_{l}")
            nc.scalar.copy(t[:], dealt(c1[l]))
            c1s.append(t)
        turn(bT[0], n0[0], True, False)
        turn(bT[0], c1s[0], False, True)
        turn(bT[1], c1s[1], True, False)
        turn(bT[1], n0[1], False, True)
        f0 = [product(f"f0_{l}", f"A{l}", w1q, g[:], half(xsg, l)) for l, g in enumerate((xwg0, xwg1))]
        ub = []
        for l in range(HALVES):
            ab = sb.tile([P, S], F32, name=f"ab_{l}")
            nc.scalar.activation(ab[:], bT[l][:], ACT.Abs)
            t = sb.tile([P, S], F32, name=f"ub_{l}")
            nc.gpsimd.tensor_scalar(t[:], ab[:], 1.0, FLOOR, ALU.mult, ALU.add)
            ub.append(t)
        parts = sb.tile([P, 2, HALVES, D], F32, name="parts", tag="ab_0")
        dinv = sb.tile([P, HALVES, D], F32, name="dinv")
        usign = sb.tile([P, HALVES, D], F32, name="usign")
        r = sb.tile([P, HALVES, D], F32, name="r")
        nc.scalar.activation(parts[:, 0], dist_v[:], ACT.Abs_reciprocal_sqrt)
        nc.scalar.activation(parts[:, 1], dist_v[:], ACT.Sign)
        nc.scalar.activation(dinv[:], parts[:, 0], ACT.Square)
        nc.gpsimd.tensor_tensor(usign[:], use_v[:], parts[:, 1], ALU.mult)
        nc.gpsimd.tensor_tensor(r[:], usign[:], dinv[:], ALU.mult)
        a, aT = [], []
        PAIRS = 2
        W = D // PAIRS
        for l in range(HALVES):
            t = sb.tile([P, D, P], F32, name=f"a_{l}")
            for g in range(PAIRS):
                ds_ = range(g * W, (g + 1) * W)
                nc.vector.tensor_tensor(t[:, g * W : (g + 1) * W], dealt(f0[l])[:, g * W : (g + 1) * W], n0[l][:, g * W : (g + 1) * W], ALU.add)
                b = bank(f"aT{l}_{g}", f"{'BC'[l]}{g}", W * P)
                turn(b, t, True, True, ds_, g * W)
                aT.append(b)
            a.append(t)
        for l in range(HALVES):
            turn(sT[l], a[l], True, False)
            turn(sT[l], c1s[l], False, True)
        roots = []
        for l in range(HALVES):
            for g in range(PAIRS):
                gc = slice(g * W * P, (g + 1) * W * P)
                aa = sb.tile([P, W * P], F32, name=f"aa_{l}_{g}")
                nc.scalar.activation(aa[:], aT[l * PAIRS + g][:], ACT.Abs)
                cost = sb.tile([P, W * P], F32, name=f"cost_{l}_{g}")
                nc.vector.scalar_tensor_tensor(cost[:], aa[:], FLOOR, ub[l][:, gc], ALU.add, ALU.mult)
                z = sb.tile([P, W * P], F32, name=f"z_{l}_{g}")
                nc.scalar.activation(z[:], cost[:], ACT.Abs_reciprocal_sqrt)
                roots.append(z)

        def add_up(name, tag, src):
            dst = bank(name, tag, P)
            for d in range(D):
                nc.tensor.matmul(out=dst[:], lhsT=src[:, d * P : (d + 1) * P], rhs=ident[:], is_transpose=True,
                                 start=d == 0, stop=d == D - 1)
            return dst

        iws, dens, nums = [], [], []
        for l in range(HALVES):
            iw = sb.tile([P, S], F32, name=f"iw_{l}")
            for d in range(D):
                zc = roots[l * PAIRS + d // W][:, (d % W) * P : (d % W + 1) * P]
                nc.vector.scalar_tensor_tensor(iw[:, d * P : (d + 1) * P], zc, r[:, l, d : d + 1], zc, ALU.mult, ALU.mult)
            iws.append(iw)
            dens.append(add_up(f"den{l}", f"A{l}", iw))
        for l in range(HALVES):
            wf = sb.tile([P, S], F32, name=f"wf_{l}")
            for g in range(l + 1):
                gc = slice(g * S // (l + 1), (g + 1) * S // (l + 1))
                nc.vector.tensor_tensor(wf[:, gc], sT[l][:, gc], iws[l][:, gc], ALU.mult)
            nums.append(add_up(f"num{l}", f"B{l}", wf))
        sums = list(zip(dens, nums))
        out_v = out.rearrange("(h m) v -> m h v", h=2)
        for l in range(HALVES):
            den, num = sums[l]
            sg = sb.tile([P, P], F32, name=f"sg_{l}")
            y = sb.tile([P, P], F32, name=f"y_{l}")
            y2 = sb.tile([P, P], F32, name=f"y2_{l}")
            nc.scalar.activation(y[:], den[:], ACT.Abs_reciprocal_sqrt)
            nc.scalar.activation(sg[:], den[:], ACT.Sign)
            nc.scalar.activation(y2[:], y[:], ACT.Square)
            t = sb.tile([P, P], F32, name=f"t_{l}")
            nc.vector.tensor_tensor(t[:], num[:], sg[:], ALU.mult)
            o = sb.tile([P, P], F32, name=f"o_{l}")
            nc.vector.scalar_tensor_tensor(o[:], t[:], 0.0, y2[:], ALU.max, ALU.mult)
            nc.sync.dma_start(out=out_v[:, :, l * VH : (l + 1) * VH], in_=o[:].rearrange("p (h v) -> p h v", h=2))
